import numpy as np
import ml_dtypes


def mxq(x, axis, fmt="e4m3"):
    dtype, down = {"e4m3": (ml_dtypes.float8_e4m3fn, 7), "e5m2": (ml_dtypes.float8_e5m2, 14)}[fmt]
    v = np.moveaxis(np.asarray(x, np.float32).astype(ml_dtypes.bfloat16).astype(np.float64), axis, -1)
    blocks = v.reshape(v.shape[:-1] + (-1, 32))
    amax = np.abs(blocks).max(-1, keepdims=True)
    byte = np.maximum(np.where(amax > 0, np.frexp(amax)[1] - 1 + 127, 0) - down, 1)
    scale = np.exp2(byte - 127.0)
    codes = (blocks / scale).astype(np.float32).astype(dtype).astype(np.float64)
    return np.moveaxis((codes * scale).reshape(v.shape), -1, axis)


WIDE = False


def mx_kscale(k):
    if not WIDE:
        return np.ones(k)
    levels = np.array([10, -10, 5, -5, 0])
    if k % 512:
        return np.exp2(np.random.permutation(np.resize(levels, k // 32))).repeat(32)
    a = np.empty((k // 512, 16))
    for p in range(k // 512):
        a[p, :8] = np.random.permutation(np.resize(levels, 8))
        for g in range(8):
            far = levels[np.abs(levels - a[p, g]) >= 10]
            a[p, g + 8] = far[np.random.randint(len(far))]
    return np.exp2(a.ravel()).repeat(32)


def f64(x):
    return np.asarray(x).astype(np.float64)


def striped(idx):
    return np.tile(idx.reshape(-1, 16).T, (8, 1)).astype(np.uint16)


def unstriped(offs):
    return offs[:16].T.reshape(-1).astype(np.int64)


def striped8(idx):
    return np.concatenate([x.reshape(-1, 16).T for x in idx]).astype(np.uint16)


def runs(offs, k):
    lists = np.stack([offs[16 * r : 16 * r + 16].T.reshape(-1) for r in range(8)]).astype(np.int64)
    return lists[np.arange(k) % 512 // 64]


def pack_weight(w):
    k, n = w.shape
    w = f64(np.asarray(w, np.float32).astype(ml_dtypes.bfloat16)).reshape(k // 32, 32, n)
    amax = np.abs(w).max(1)
    byte = np.clip(np.where(amax > 0, np.frexp(amax)[1] - 1 + 127 - 7, 1), 1, 254)
    scaled = (w * np.exp2(127.0 - byte)[:, None, :]).reshape(k, n).astype(np.float32)
    words = np.ascontiguousarray(scaled.reshape(k // 512, 128, 4, n).transpose(0, 1, 3, 2)).astype(ml_dtypes.float8_e4m3fn).view(np.uint8)
    return words, np.ascontiguousarray(byte.astype(np.uint8).reshape(k // 512, 16, n))


def unpack_weight(words, scales):
    g, p, n, _ = words.shape
    vals = np.ascontiguousarray(words).view(ml_dtypes.float8_e4m3fn).astype(np.float64) * np.repeat(np.exp2(scales.astype(np.float64) - 127.0), 8, axis=1)[..., None]
    return vals.transpose(0, 1, 3, 2).reshape(g * 512, n)


def sigmoid(v):
    return 1.0 / (1.0 + np.exp(-np.maximum(v, -700.0)))

def planes(y):
    n, m = y.shape
    v = y.astype(np.float32).astype(ml_dtypes.bfloat16).astype(np.float64).reshape(n // 32, 32, m)
    top = np.abs(v).max(1)
    byte = np.clip(np.where(top > 0, np.frexp(top)[1] - 1 + 127 - 7, 1), 1, 254)
    codes = (v * np.exp2(127.0 - byte)[:, None, :]).reshape(n, m).astype(np.float32).astype(ml_dtypes.float8_e4m3fn).view(np.uint8)
    words = codes.reshape(n // 512, 128, 4, m).transpose(0, 1, 3, 2)
    return np.ascontiguousarray(words), np.ascontiguousarray(byte.astype(np.uint8).reshape(n // 512, 16, m))


K, T, S, H, C = 512, 2048, 512, 512, 512


def setup_inputs():
    n = np.random.standard_normal
    s = mx_kscale(K)[:, None]
    packed_xT = pack_weight(n((K, T)) * s)
    packed_w1 = pack_weight(n((K, H)) / np.sqrt(K) / s)
    packed_w2 = pack_weight(n((K, H)) / np.sqrt(K) / s)
    return {
        "x_words": packed_xT[0],
        "x_scales": packed_xT[1],
        "w1_words": packed_w1[0],
        "w1_scales": packed_w1[1],
        "w2_words": packed_w2[0],
        "w2_scales": packed_w2[1],
        "sl": np.random.uniform(1.0, 2.0, (H, 1)).astype(np.float32),
        "th": (0.5 * n((H, 1))).astype(np.float32),
        "gs": (np.random.uniform(0.5, 1.5, (K, 1)) / s).astype(np.float32),
        "tau": np.random.uniform(0.3, 0.9, (C, 1)).astype(np.float32),
        "offs": striped(np.random.permutation(T)[:S]),
        "two": striped(np.random.permutation(T)[:S]),
        "n1": striped(np.random.permutation(S)),
        "n2": striped(np.random.permutation(S)),
        "cand": striped(np.random.permutation(T)[:C]),
        "n3": striped8(np.stack([np.random.permutation(S) for _ in range(8)])),
        "n4": striped8(np.stack([np.random.permutation(S) for _ in range(8)])),
    }


def reference(x_words, x_scales, w1_words, w1_scales, w2_words, w2_scales, sl, th, gs, tau, offs, two, n1, n2, cand, n3, n4):
    x_cand = unpack_weight(x_words, x_scales)[:, unstriped(cand)]
    xq = unpack_weight(x_words, x_scales)[:, unstriped(offs)]
    y = unpack_weight(w1_words, w1_scales).T @ xq
    x_two = unpack_weight(x_words, x_scales)[:, unstriped(two)]
    d = unpack_weight(w2_words, w2_scales).T @ x_two
    sg = sigmoid(f64(sl) * (d[:, unstriped(n1)] - f64(th)))
    z = f64(gs) * (np.maximum(y * sg, d[:, unstriped(n2)] - d))
    s = 0.0625 * ((x_cand.T @ mxq(z, 0, "e4m3")))
    top = s.max(axis=1, keepdims=True)
    ea = np.exp(f64(tau) * (s[np.arange(C)[:, None], runs(n4, C)] - top))
    out_0 = (0.5 * (s - (s[np.arange(C)[:, None], runs(n3, C)]))) / (ea + 0.25)
    return (out_0,) + planes(out_0)

@@ -1,0 +1,221 @@
+from contextlib import ExitStack
+
+import concourse.mybir as mybir
+
+K, T, S, H, C = 512, 2048, 512, 512, 512
+FLOPS = 2 * K * (2 * H * S + C * S)
+
+F32 = mybir.dt.float32
+BF16 = mybir.dt.bfloat16
+I32 = mybir.dt.int32
+U32 = mybir.dt.uint32
+U16 = mybir.dt.uint16
+U8 = mybir.dt.uint8
+FP8X4 = mybir.dt.float8_e4m3fn_x4
+ALU = mybir.AluOpType
+ACT = mybir.ActivationFunctionType
+
+P = 128
+PACK = 4
+HALF = S // 2
+LCOLS = HALF // 16
+QUARTER = S // 4
+
+
+def tile_picked_twcmxbera_none_po_kernel(
+    tc, x_words, x_scales, w1_words, w1_scales, w2_words, w2_scales, sl, th, gs, tau,
+    offs, two, n1, n2, cand, n3, n4, out_0, out_1, out_2,
+):
+    nc = tc.nc
+    with ExitStack() as ctx:
+        keep = ctx.enter_context(tc.tile_pool(name="keep", bufs=1))
+        psum = ctx.enter_context(tc.psum_pool(name="psum", bufs=1))
+
+        def sb(name, shape, dtype):
+            return keep.tile(shape, dtype, name=name, align_bytes=64)
+
+        def load_list(name, src):
+            lst = keep.tile([P, S // 16], U16, name=name)
+            nc.sync.dma_start(lst[:], src)
+            return lst
+
+        def load_words(engine, name, src, width):
+            words = sb(name, [P, width], I32)
+            engine.dma_start(words[:], src[0].rearrange("p n t -> p (n t)").bitcast(I32))
+            return words
+
+        def cleared_plane(clearer, name, width):
+            plane = sb(name, [P, width], U8)
+            clearer.memset(plane[:].bitcast(I32), 0)
+            return plane
+
+        def load_scales(engine, plane, src, quadrants):
+            for q in quadrants:
+                engine.dma_start(plane[32 * q : 32 * q + 4, :].bitcast(I32), src[0, 4 * q : 4 * q + 4, :].bitcast(I32))
+
+        def load_column(engine, name, src):
+            col = sb(name, [P, PACK], F32)
+            engine.dma_start(col[:], src.rearrange("(p t) o -> p (t o)", t=PACK))
+            return col
+
+        def dealt(ap):
+            return ap.rearrange("p (t m) -> p m t", t=PACK)
+
+        def plain(ap):
+            return ap.rearrange("p (m t) -> p m t", t=PACK)
+
+        xs = cleared_plane(nc.vector, "xs", T)
+        w2s_raw = cleared_plane(nc.vector, "w2s_raw", H)
+        w1s_raw = cleared_plane(nc.vector, "w1s_raw", H)
+        two_l = load_list("two_l", two)
+        offs_l = load_list("offs_l", offs)
+        xw = load_words(nc.sync, "xw", x_words, T)
+        load_scales(nc.sync, xs, x_scales, range(4))
+        load_scales(nc.sync, w2s_raw, w2_scales, (0, 1))
+        load_scales(nc.gpsimd, w2s_raw, w2_scales, (2, 3))
+        load_scales(nc.gpsimd, w1s_raw, w1_scales, range(4))
+        w2w_raw = load_words(nc.sync, "w2w_raw", w2_words, H)
+        n1_l = load_list("n1_l", n1)
+        sl_c = load_column(nc.sync, "sl_c", sl)
+        th_c = load_column(nc.sync, "th_c", th)
+        w1w_raw = load_words(nc.sync, "w1w_raw", w1_words, H)
+        n2_l = load_list("n2_l", n2)
+        cand_l = load_list("cand_l", cand)
+        gs_c = load_column(nc.sync, "gs_c", gs)
+        tau_c = load_column(nc.sync, "tau_c", tau)
+        n3_l = load_list("n3_l", n3)
+        n4_l = load_list("n4_l", n4)
+
+        def gather_packed(name, lst, view):
+            words = sb(name + "_w", [P, S], U32)
+            scales = sb(name + "_s", [P, S], U8)
+            nc.vector.tensor_copy(view(scales[:]), xs[:].indirect(lst[:]))
+            nc.vector.tensor_copy(view(words[:]), xw[:].bitcast(U32).indirect(lst[:]))
+            return words, scales
+
+        def deal_weight(name, words_raw, scales_raw):
+            words = sb(name + "_w", [P, H], U32)
+            scales = sb(name + "_s", [P, H], U8)
+            nc.scalar.copy(dealt(words[:]), plain(words_raw[:].bitcast(U32)))
+            nc.vector.tensor_copy(dealt(scales[:]), plain(scales_raw[:]))
+            return words, scales
+
+        def product(out, lhs, t, rhs_w, rhs_s):
+            cols = slice(P * t, P * (t + 1))
+            nc.tensor.matmul_mx(
+                out=out, lhsT=lhs[0][:, cols].bitcast(FP8X4), lhsT_scale=lhs[1][:, cols],
+                rhs=rhs_w.bitcast(FP8X4), rhs_scale=rhs_s, start=True, stop=True,
+            )
+
+        x_two = gather_packed("x_two", two_l, lambda ap: ap)
+        w2 = deal_weight("w2", w2w_raw, w2s_raw)
+
+        d_win = []
+        for t in range(PACK):
+            bank = psum.tile([P, S], F32, name="row_bank", tag="row%d" % t)
+            product(bank[:], w2, t, x_two[0][:], x_two[1][:])
+            win = sb("d_win%d" % t, [P, S], F32)
+            nc.scalar.copy(win[:], bank[:])
+            d_win.append(win)
+
+        sg_bias = sb("sg_bias", [P, PACK], F32)
+        nc.vector.scalar_tensor_tensor(sg_bias[:], sl_c[:], -1.0, th_c[:], ALU.mult, ALU.mult)
+        neg_tau = sb("neg_tau", [P, PACK], F32)
+        nc.vector.tensor_scalar(neg_tau[:], tau_c[:], -1.0, None, ALU.mult)
+
+        x_idx = gather_packed("x_idx", offs_l, lambda ap: ap)
+        w1 = deal_weight("w1", w1w_raw, w1s_raw)
+        y_banks = {}
+        for h in range(2):
+            cols = slice(HALF * h, HALF * (h + 1))
+            for u in range(2):
+                bank = psum.tile([P, 2, HALF], F32, name="y_bank", tag="y%d%d" % (h, u))
+                for e in range(2):
+                    product(bank[:, e, :], w1, 2 * u + e, x_idx[0][:, cols], x_idx[1][:, cols])
+                y_banks[h, u] = bank
+        x_cand = gather_packed("x_cand", cand_l, dealt)
+
+        s_banks = [psum.tile([P, S], F32, name="s_bank", tag="row%d" % t) for t in range(PACK)]
+        for h in range(2):
+            cols = slice(HALF * h, HALF * (h + 1))
+            lcols = slice(LCOLS * h, LCOLS * (h + 1))
+            sg = sb("sg%d" % h, [P, PACK, HALF], F32)
+            d2 = sb("d2%d" % h, [P, PACK, HALF], F32)
+            gated = sb("gated%d" % h, [P, PACK, HALF], F32)
+            delta = sb("delta%d" % h, [P, PACK, HALF], F32)
+            larger = sb("larger%d" % h, [P, PACK, HALF], F32)
+            for u in range(2):
+                pair = slice(2 * u, 2 * u + 2)
+                for t in (2 * u, 2 * u + 1):
+                    nc.scalar.activation(
+                        sg[:, t, :], d_win[t][:].indirect(n1_l[:, lcols]), ACT.Sigmoid,
+                        bias=sg_bias[:, t : t + 1], scale=sl_c[:, t : t + 1],
+                    )
+                    nc.scalar.activation(d2[:, t, :], d_win[t][:].indirect(n2_l[:, lcols]), ACT.Copy)
+                    nc.vector.tensor_tensor(delta[:, t, :], d2[:, t, :], d_win[t][:, cols], ALU.subtract)
+                nc.vector.tensor_tensor(gated[:, pair, :], y_banks[h, u][:], sg[:, pair, :], ALU.mult)
+            for u in range(2):
+                pair = slice(2 * u, 2 * u + 2)
+                nc.vector.tensor_tensor(larger[:, pair, :], gated[:, pair, :], delta[:, pair, :], ALU.max)
+            z_bf = sb("z_bf%d" % h, [P, HALF * PACK], BF16)
+            nc.vector.tensor_tensor(
+                z_bf[:].rearrange("p (c i t) -> p c t i", i=4, t=PACK),
+                larger[:].rearrange("p t (c i) -> p c t i", i=4),
+                gs_c[:].unsqueeze(1).unsqueeze(3).to_broadcast([P, HALF // 4, PACK, 4]),
+                ALU.mult,
+            )
+            z_w = sb("z_w%d" % h, [P, HALF], U32)
+            z_s = sb("z_s%d" % h, [P, HALF], U8)
+            nc.vector.quantize_mx(out=z_w[:].bitcast(FP8X4), scales=z_s[:], in_=z_bf[:])
+            for t in range(PACK):
+                product(s_banks[t][:, cols], x_cand, t, z_w[:], z_s[:])
+
+        top = sb("top", [P, PACK], F32)
+        ea_bias = sb("ea_bias", [P, PACK], F32)
+        ea = sb("ea", [P, PACK, S], F32)
+        s3 = sb("s3", [P, PACK, S], F32)
+        diff = sb("diff", [P, PACK, S], F32)
+        s_win = []
+        for t in range(PACK):
+            win = sb("s_win%d" % t, [P, S], F32)
+            nc.vector.tensor_scalar(win[:], s_banks[t][:], 0.0625, None, ALU.mult, ALU.max, accum_out=top[:, t : t + 1])
+            s_win.append(win)
+            nc.scalar.activation(ea_bias[:, t : t + 1], top[:, t : t + 1], ACT.Copy, scale=neg_tau[:, t : t + 1])
+            for h in range(2):
+                cols = slice(HALF * h, HALF * (h + 1))
+                lcols = slice(LCOLS * h, LCOLS * (h + 1))
+                nc.scalar.activation(
+                    ea[:, t, cols], win[:].indirect(n4_l[:, lcols]), ACT.Exp,
+                    bias=ea_bias[:, t : t + 1], scale=tau_c[:, t : t + 1],
+                )
+        for t in range(PACK):
+            for h in range(2):
+                cols = slice(HALF * h, HALF * (h + 1))
+                lcols = slice(LCOLS * h, LCOLS * (h + 1))
+                nc.vector.tensor_copy(s3[:, t, cols], s_win[t][:].indirect(n3_l[:, lcols]))
+        for t in range(PACK):
+            nc.vector.tensor_tensor(diff[:, t, :], s_win[t][:], s3[:, t, :], ALU.subtract)
+
+        out_rows = out_0.rearrange("(p t) n -> p t n", t=PACK)
+        words_out = out_1[0].rearrange("p n t -> p (n t)").bitcast(I32)
+        o_s = sb("o_s", [P, S], U8)
+        for c in range(4):
+            cols = slice(QUARTER * c, QUARTER * (c + 1))
+            root = sb("root%d" % c, [P, PACK, QUARTER], F32)
+            recip = sb("recip%d" % c, [P, PACK, QUARTER], F32)
+            res = sb("res%d" % c, [P, PACK, QUARTER], F32)
+            nc.scalar.activation(root[:], ea[:, :, cols], ACT.Abs_reciprocal_sqrt, bias=0.5, scale=2.0)
+            nc.scalar.activation(recip[:], root[:], ACT.Square)
+            nc.vector.tensor_tensor(res[:], diff[:, :, cols], recip[:], ALU.mult)
+            nc.sync.dma_start(out_rows[:, :, cols], res[:])
+            o_bf = sb("o_bf%d" % c, [P, QUARTER * PACK], BF16)
+            nc.vector.tensor_copy(
+                o_bf[:].rearrange("p (c i t) -> p c t i", i=4, t=PACK),
+                res[:].rearrange("p t (c i) -> p c t i", i=4),
+            )
+            o_w = sb("o_w%d" % c, [P, QUARTER], I32)
+            nc.vector.quantize_mx(out=o_w[:].bitcast(FP8X4), scales=o_s[:, cols], in_=o_bf[:])
+            nc.scalar.dma_start(words_out[:, cols], o_w[:])
+        for q in range(4):
+            engine = nc.sync if q % 2 else nc.scalar
+            engine.dma_start(out_2[0, 4 * q : 4 * q + 4, :].bitcast(I32), o_s[32 * q : 32 * q + 4, :].bitcast(I32))

@@ -44,14 +44,14 @@ def tile_picked_twcmxbera_none_po_kernel(
             engine.dma_start(words[:], src[0].rearrange("p n t -> p (n t)").bitcast(I32))
             return words
 
-        def cleared_plane(clearer, name, width):
+        def load_scales(name, src, width, engines):
             plane = sb(name, [P, width], U8)
-            clearer.memset(plane[:].bitcast(I32), 0)
+            for q, engine in enumerate(engines):
+                rows = src[0, 4 * q : 4 * q + 4, :].bitcast(I32)
+                engine.dma_start(
+                    plane[32 * q : 32 * q + 32, :].bitcast(I32), rows.unsqueeze(0).to_broadcast([8, 4, width // 4])
+                )
             return plane
-
-        def load_scales(engine, plane, src, quadrants):
-            for q in quadrants:
-                engine.dma_start(plane[32 * q : 32 * q + 4, :].bitcast(I32), src[0, 4 * q : 4 * q + 4, :].bitcast(I32))
 
         def load_column(engine, name, src):
             col = sb(name, [P, PACK], F32)
@@ -64,40 +64,41 @@ def tile_picked_twcmxbera_none_po_kernel(
         def plain(ap):
             return ap.rearrange("p (m t) -> p m t", t=PACK)
 
-        xs = cleared_plane(nc.vector, "xs", T)
-        w2s_raw = cleared_plane(nc.vector, "w2s_raw", H)
-        w1s_raw = cleared_plane(nc.vector, "w1s_raw", H)
         two_l = load_list("two_l", two)
+        xs = load_scales("xs", x_scales, T, (nc.scalar, nc.scalar, nc.scalar, nc.sync))
         offs_l = load_list("offs_l", offs)
         xw = load_words(nc.sync, "xw", x_words, T)
-        load_scales(nc.sync, xs, x_scales, range(4))
-        load_scales(nc.sync, w2s_raw, w2_scales, (0, 1))
-        load_scales(nc.gpsimd, w2s_raw, w2_scales, (2, 3))
-        load_scales(nc.gpsimd, w1s_raw, w1_scales, range(4))
-        w2w_raw = load_words(nc.sync, "w2w_raw", w2_words, H)
-        n1_l = load_list("n1_l", n1)
+        w2w_raw = load_words(nc.scalar, "w2w_raw", w2_words, H)
+        w2s_raw = load_scales("w2s_raw", w2_scales, H, [nc.sync] * 4)
         sl_c = load_column(nc.sync, "sl_c", sl)
         th_c = load_column(nc.sync, "th_c", th)
-        w1w_raw = load_words(nc.sync, "w1w_raw", w1_words, H)
-        n2_l = load_list("n2_l", n2)
+        n1_l = load_list("n1_l", n1)
         cand_l = load_list("cand_l", cand)
+        n2_l = load_list("n2_l", n2)
+        w1w_raw = load_words(nc.sync, "w1w_raw", w1_words, H)
+        w1s_raw = load_scales("w1s_raw", w1_scales, H, [nc.sync] * 4)
         gs_c = load_column(nc.sync, "gs_c", gs)
         tau_c = load_column(nc.sync, "tau_c", tau)
         n3_l = load_list("n3_l", n3)
         n4_l = load_list("n4_l", n4)
 
-        def gather_packed(name, lst, view):
-            words = sb(name + "_w", [P, S], U32)
-            scales = sb(name + "_s", [P, S], U8)
+        def gather_scales(name, lst, view):
+            scales = sb(name, [P, S], U8)
             nc.vector.tensor_copy(view(scales[:]), xs[:].indirect(lst[:]))
-            nc.vector.tensor_copy(view(words[:]), xw[:].bitcast(U32).indirect(lst[:]))
-            return words, scales
+            return scales
 
-        def deal_weight(name, words_raw, scales_raw):
+        def gather_words(name, lst, view):
+            words = sb(name, [P, S], U32)
+            nc.vector.tensor_copy(view(words[:]), xw[:].bitcast(U32).indirect(lst[:]))
+            return words
+
+        def deal_weight(name, words_raw, scales_raw, copy_words):
             words = sb(name + "_w", [P, H], U32)
             scales = sb(name + "_s", [P, H], U8)
-            nc.scalar.copy(dealt(words[:]), plain(words_raw[:].bitcast(U32)))
-            nc.vector.tensor_copy(dealt(scales[:]), plain(scales_raw[:]))
+            copy_words(dealt(words[:]), plain(words_raw[:].bitcast(U32)))
+            nc.gpsimd.tensor_copy(
+                scales[:].rearrange("p (t m) -> p t m", t=PACK), scales_raw[:].rearrange("p (m t) -> p t m", t=PACK)
+            )
             return words, scales
 
         def product(out, lhs, t, rhs_w, rhs_s):
@@ -107,8 +108,11 @@ def tile_picked_twcmxbera_none_po_kernel(
                 rhs=rhs_w.bitcast(FP8X4), rhs_scale=rhs_s, start=True, stop=True,
             )
 
-        x_two = gather_packed("x_two", two_l, lambda ap: ap)
-        w2 = deal_weight("w2", w2w_raw, w2s_raw)
+        two_s = gather_scales("two_s", two_l, lambda ap: ap)
+        idx_s = gather_scales("idx_s", offs_l, lambda ap: ap)
+        x_two = (gather_words("two_w", two_l, lambda ap: ap), two_s)
+        x_idx = (gather_words("idx_w", offs_l, lambda ap: ap), idx_s)
+        w2 = deal_weight("w2", w2w_raw, w2s_raw, nc.scalar.copy)
 
         d_win = []
         for t in range(PACK):
@@ -121,10 +125,9 @@ def tile_picked_twcmxbera_none_po_kernel(
         sg_bias = sb("sg_bias", [P, PACK], F32)
         nc.vector.scalar_tensor_tensor(sg_bias[:], sl_c[:], -1.0, th_c[:], ALU.mult, ALU.mult)
         neg_tau = sb("neg_tau", [P, PACK], F32)
-        nc.vector.tensor_scalar(neg_tau[:], tau_c[:], -1.0, None, ALU.mult)
+        nc.gpsimd.tensor_scalar(neg_tau[:], tau_c[:], -1.0, 1.0, ALU.mult, ALU.mult)
 
-        x_idx = gather_packed("x_idx", offs_l, lambda ap: ap)
-        w1 = deal_weight("w1", w1w_raw, w1s_raw)
+        w1 = deal_weight("w1", w1w_raw, w1s_raw, nc.gpsimd.tensor_copy)
         y_banks = {}
         for h in range(2):
             cols = slice(HALF * h, HALF * (h + 1))
@@ -133,16 +136,17 @@ def tile_picked_twcmxbera_none_po_kernel(
                 for e in range(2):
                     product(bank[:, e, :], w1, 2 * u + e, x_idx[0][:, cols], x_idx[1][:, cols])
                 y_banks[h, u] = bank
-        x_cand = gather_packed("x_cand", cand_l, dealt)
+        cand_s = gather_scales("cand_s", cand_l, dealt)
+        x_cand = (gather_words("cand_w", cand_l, dealt), cand_s)
 
-        s_banks = [psum.tile([P, S], F32, name="s_bank", tag="row%d" % t) for t in range(PACK)]
+        s_banks = {}
         for h in range(2):
             cols = slice(HALF * h, HALF * (h + 1))
             lcols = slice(LCOLS * h, LCOLS * (h + 1))
             sg = sb("sg%d" % h, [P, PACK, HALF], F32)
             d2 = sb("d2%d" % h, [P, PACK, HALF], F32)
-            gated = sb("gated%d" % h, [P, PACK, HALF], F32)
-            delta = sb("delta%d" % h, [P, PACK, HALF], F32)
+            gated = sb("gated", [P, PACK, HALF], F32)
+            delta = sb("delta", [P, PACK, HALF], F32)
             larger = sb("larger%d" % h, [P, PACK, HALF], F32)
             for u in range(2):
                 pair = slice(2 * u, 2 * u + 2)
@@ -151,7 +155,10 @@ def tile_picked_twcmxbera_none_po_kernel(
                         sg[:, t, :], d_win[t][:].indirect(n1_l[:, lcols]), ACT.Sigmoid,
                         bias=sg_bias[:, t : t + 1], scale=sl_c[:, t : t + 1],
                     )
-                    nc.scalar.activation(d2[:, t, :], d_win[t][:].indirect(n2_l[:, lcols]), ACT.Copy)
+                    if h == 0 and t >= 2:
+                        nc.vector.tensor_copy(d2[:, t, :], d_win[t][:].indirect(n2_l[:, lcols]))
+                    else:
+                        nc.scalar.activation(d2[:, t, :], d_win[t][:].indirect(n2_l[:, lcols]), ACT.Copy)
                     nc.vector.tensor_tensor(delta[:, t, :], d2[:, t, :], d_win[t][:, cols], ALU.subtract)
                 nc.vector.tensor_tensor(gated[:, pair, :], y_banks[h, u][:], sg[:, pair, :], ALU.mult)
             for u in range(2):
@@ -167,20 +174,36 @@ def tile_picked_twcmxbera_none_po_kernel(
             z_w = sb("z_w%d" % h, [P, HALF], U32)
             z_s = sb("z_s%d" % h, [P, HALF], U8)
             nc.vector.quantize_mx(out=z_w[:].bitcast(FP8X4), scales=z_s[:], in_=z_bf[:])
-            for t in range(PACK):
-                product(s_banks[t][:, cols], x_cand, t, z_w[:], z_s[:])
+            for u in range(2):
+                bank = psum.tile([P, 2, HALF], F32, name="s_bank", tag="row%d" % (2 * h + u))
+                for e in range(2):
+                    product(bank[:, e, :], x_cand, 2 * u + e, z_w[:], z_s[:])
+                s_banks[h, u] = bank
 
         top = sb("top", [P, PACK], F32)
         ea_bias = sb("ea_bias", [P, PACK], F32)
         ea = sb("ea", [P, PACK, S], F32)
         s3 = sb("s3", [P, PACK, S], F32)
         diff = sb("diff", [P, PACK, S], F32)
-        s_win = []
+        half_top = sb("half_top", [P, PACK], F32)
+        s_win = [sb("s_win%d" % t, [P, S], F32) for t in range(PACK)]
+
+        def first_half(t):
+            nc.vector.tensor_scalar(
+                s_win[t][:, :HALF], s_banks[0, t // 2][:, t % 2, :], 0.0625, None, ALU.mult, ALU.max,
+                accum_out=half_top[:, t : t + 1],
+            )
+
+        first_half(0)
         for t in range(PACK):
-            win = sb("s_win%d" % t, [P, S], F32)
-            nc.vector.tensor_scalar(win[:], s_banks[t][:], 0.0625, None, ALU.mult, ALU.max, accum_out=top[:, t : t + 1])
-            s_win.append(win)
-            nc.scalar.activation(ea_bias[:, t : t + 1], top[:, t : t + 1], ACT.Copy, scale=neg_tau[:, t : t + 1])
+            if t + 1 < PACK:
+                first_half(t + 1)
+            win = s_win[t]
+            nc.vector.tensor_scalar(
+                win[:, HALF:], s_banks[1, t // 2][:, t % 2, :], 0.0625, half_top[:, t : t + 1], ALU.mult, ALU.max,
+                accum_out=top[:, t : t + 1],
+            )
+            nc.gpsimd.tensor_tensor(ea_bias[:, t : t + 1], top[:, t : t + 1], neg_tau[:, t : t + 1], ALU.mult)
             for h in range(2):
                 cols = slice(HALF * h, HALF * (h + 1))
                 lcols = slice(LCOLS * h, LCOLS * (h + 1))

from contextlib import ExitStack

import concourse.mybir as mybir

K, T, S, H, C = 512, 2048, 512, 512, 512
FLOPS = 2 * K * (2 * H * S + C * S)

F32 = mybir.dt.float32
BF16 = mybir.dt.bfloat16
I32 = mybir.dt.int32
U32 = mybir.dt.uint32
U16 = mybir.dt.uint16
U8 = mybir.dt.uint8
FP8X4 = mybir.dt.float8_e4m3fn_x4
ALU = mybir.AluOpType
ACT = mybir.ActivationFunctionType

P = 128
PACK = 4
HALF = S // 2
LCOLS = HALF // 16
QUARTER = S // 4


def tile_picked_twcmxbera_none_po_kernel(
    tc, x_words, x_scales, w1_words, w1_scales, w2_words, w2_scales, sl, th, gs, tau,
    offs, two, n1, n2, cand, n3, n4, out_0, out_1, out_2,
):
    nc = tc.nc
    with ExitStack() as ctx:
        keep = ctx.enter_context(tc.tile_pool(name="keep", bufs=1))
        psum = ctx.enter_context(tc.psum_pool(name="psum", bufs=1))

        def sb(name, shape, dtype):
            return keep.tile(shape, dtype, name=name, align_bytes=64)

        def load_list(name, src):
            lst = keep.tile([P, S // 16], U16, name=name)
            nc.sync.dma_start(lst[:], src)
            return lst

        def load_words(engine, name, src, width):
            words = sb(name, [P, width], I32)
            engine.dma_start(words[:], src[0].rearrange("p n t -> p (n t)").bitcast(I32))
            return words

        def load_scales(name, src, width, engines):
            plane = sb(name, [P, width], U8)
            for q, engine in enumerate(engines):
                rows = src[0, 4 * q : 4 * q + 4, :].bitcast(I32)
                engine.dma_start(
                    plane[32 * q : 32 * q + 32, :].bitcast(I32), rows.unsqueeze(0).to_broadcast([8, 4, width // 4])
                )
            return plane

        def load_column(engine, name, src):
            col = sb(name, [P, PACK], F32)
            engine.dma_start(col[:], src.rearrange("(p t) o -> p (t o)", t=PACK))
            return col

        def dealt(ap):
            return ap.rearrange("p (t m) -> p m t", t=PACK)

        def plain(ap):
            return ap.rearrange("p (m t) -> p m t", t=PACK)

        two_l = load_list("two_l", two)
        xs = load_scales("xs", x_scales, T, (nc.scalar, nc.scalar, nc.scalar, nc.sync))
        offs_l = load_list("offs_l", offs)
        xw = load_words(nc.sync, "xw", x_words, T)
        w2w_raw = load_words(nc.scalar, "w2w_raw", w2_words, H)
        w2s_raw = load_scales("w2s_raw", w2_scales, H, [nc.sync] * 4)
        sl_c = load_column(nc.sync, "sl_c", sl)
        th_c = load_column(nc.sync, "th_c", th)
        n1_l = load_list("n1_l", n1)
        cand_l = load_list("cand_l", cand)
        n2_l = load_list("n2_l", n2)
        w1w_raw = load_words(nc.sync, "w1w_raw", w1_words, H)
        w1s_raw = load_scales("w1s_raw", w1_scales, H, [nc.sync] * 4)
        gs_c = load_column(nc.sync, "gs_c", gs)
        tau_c = load_column(nc.sync, "tau_c", tau)
        n3_l = load_list("n3_l", n3)
        n4_l = load_list("n4_l", n4)

        def gather_scales(name, lst, view):
            scales = sb(name, [P, S], U8)
            nc.vector.tensor_copy(view(scales[:]), xs[:].indirect(lst[:]))
            return scales

        def gather_words(name, lst, view):
            words = sb(name, [P, S], U32)
            nc.vector.tensor_copy(view(words[:]), xw[:].bitcast(U32).indirect(lst[:]))
            return words

        def deal_weight(name, words_raw, scales_raw, copy_words):
            words = sb(name + "_w", [P, H], U32)
            scales = sb(name + "_s", [P, H], U8)
            copy_words(dealt(words[:]), plain(words_raw[:].bitcast(U32)))
            nc.gpsimd.tensor_copy(
                scales[:].rearrange("p (t m) -> p t m", t=PACK), scales_raw[:].rearrange("p (m t) -> p t m", t=PACK)
            )
            return words, scales

        def product(out, lhs, t, rhs_w, rhs_s):
            cols = slice(P * t, P * (t + 1))
            nc.tensor.matmul_mx(
                out=out, lhsT=lhs[0][:, cols].bitcast(FP8X4), lhsT_scale=lhs[1][:, cols],
                rhs=rhs_w.bitcast(FP8X4), rhs_scale=rhs_s, start=True, stop=True,
            )

        two_s = gather_scales("two_s", two_l, lambda ap: ap)
        idx_s = gather_scales("idx_s", offs_l, lambda ap: ap)
        x_two = (gather_words("two_w", two_l, lambda ap: ap), two_s)
        x_idx = (gather_words("idx_w", offs_l, lambda ap: ap), idx_s)
        w2 = deal_weight("w2", w2w_raw, w2s_raw, nc.scalar.copy)

        d_win = []
        for t in range(PACK):
            bank = psum.tile([P, S], F32, name="row_bank", tag="row%d" % t)
            product(bank[:], w2, t, x_two[0][:], x_two[1][:])
            win = sb("d_win%d" % t, [P, S], F32)
            nc.scalar.copy(win[:], bank[:])
            d_win.append(win)

        sg_bias = sb("sg_bias", [P, PACK], F32)
        nc.vector.scalar_tensor_tensor(sg_bias[:], sl_c[:], -1.0, th_c[:], ALU.mult, ALU.mult)
        neg_tau = sb("neg_tau", [P, PACK], F32)
        nc.gpsimd.tensor_scalar(neg_tau[:], tau_c[:], -1.0, 1.0, ALU.mult, ALU.mult)

        w1 = deal_weight("w1", w1w_raw, w1s_raw, nc.gpsimd.tensor_copy)
        y_banks = {}
        for h in range(2):
            cols = slice(HALF * h, HALF * (h + 1))
            for u in range(2):
                bank = psum.tile([P, 2, HALF], F32, name="y_bank", tag="y%d%d" % (h, u))
                for e in range(2):
                    product(bank[:, e, :], w1, 2 * u + e, x_idx[0][:, cols], x_idx[1][:, cols])
                y_banks[h, u] = bank
        cand_s = gather_scales("cand_s", cand_l, dealt)
        x_cand = (gather_words("cand_w", cand_l, dealt), cand_s)

        s_banks = {}
        for h in range(2):
            cols = slice(HALF * h, HALF * (h + 1))
            lcols = slice(LCOLS * h, LCOLS * (h + 1))
            sg = sb("sg%d" % h, [P, PACK, HALF], F32)
            d2 = sb("d2%d" % h, [P, PACK, HALF], F32)
            gated = sb("gated", [P, PACK, HALF], F32)
            delta = sb("delta", [P, PACK, HALF], F32)
            larger = sb("larger%d" % h, [P, PACK, HALF], F32)
            for u in range(2):
                pair = slice(2 * u, 2 * u + 2)
                for t in (2 * u, 2 * u + 1):
                    nc.scalar.activation(
                        sg[:, t, :], d_win[t][:].indirect(n1_l[:, lcols]), ACT.Sigmoid,
                        bias=sg_bias[:, t : t + 1], scale=sl_c[:, t : t + 1],
                    )
                    if h == 0 and t >= 2:
                        nc.vector.tensor_copy(d2[:, t, :], d_win[t][:].indirect(n2_l[:, lcols]))
                    else:
                        nc.scalar.activation(d2[:, t, :], d_win[t][:].indirect(n2_l[:, lcols]), ACT.Copy)
                    nc.vector.tensor_tensor(delta[:, t, :], d2[:, t, :], d_win[t][:, cols], ALU.subtract)
                nc.vector.tensor_tensor(gated[:, pair, :], y_banks[h, u][:], sg[:, pair, :], ALU.mult)
            for u in range(2):
                pair = slice(2 * u, 2 * u + 2)
                nc.vector.tensor_tensor(larger[:, pair, :], gated[:, pair, :], delta[:, pair, :], ALU.max)
            z_bf = sb("z_bf%d" % h, [P, HALF * PACK], BF16)
            nc.vector.tensor_tensor(
                z_bf[:].rearrange("p (c i t) -> p c t i", i=4, t=PACK),
                larger[:].rearrange("p t (c i) -> p c t i", i=4),
                gs_c[:].unsqueeze(1).unsqueeze(3).to_broadcast([P, HALF // 4, PACK, 4]),
                ALU.mult,
            )
            z_w = sb("z_w%d" % h, [P, HALF], U32)
            z_s = sb("z_s%d" % h, [P, HALF], U8)
            nc.vector.quantize_mx(out=z_w[:].bitcast(FP8X4), scales=z_s[:], in_=z_bf[:])
            for u in range(2):
                bank = psum.tile([P, 2, HALF], F32, name="s_bank", tag="row%d" % (2 * h + u))
                for e in range(2):
                    product(bank[:, e, :], x_cand, 2 * u + e, z_w[:], z_s[:])
                s_banks[h, u] = bank

        top = sb("top", [P, PACK], F32)
        ea_bias = sb("ea_bias", [P, PACK], F32)
        ea = sb("ea", [P, PACK, S], F32)
        s3 = sb("s3", [P, PACK, S], F32)
        diff = sb("diff", [P, PACK, S], F32)
        half_top = sb("half_top", [P, PACK], F32)
        s_win = [sb("s_win%d" % t, [P, S], F32) for t in range(PACK)]

        def first_half(t):
            nc.vector.tensor_scalar(
                s_win[t][:, :HALF], s_banks[0, t // 2][:, t % 2, :], 0.0625, None, ALU.mult, ALU.max,
                accum_out=half_top[:, t : t + 1],
            )

        first_half(0)
        for t in range(PACK):
            if t + 1 < PACK:
                first_half(t + 1)
            win = s_win[t]
            nc.vector.tensor_scalar(
                win[:, HALF:], s_banks[1, t // 2][:, t % 2, :], 0.0625, half_top[:, t : t + 1], ALU.mult, ALU.max,
                accum_out=top[:, t : t + 1],
            )
            nc.gpsimd.tensor_tensor(ea_bias[:, t : t + 1], top[:, t : t + 1], neg_tau[:, t : t + 1], ALU.mult)
            for h in range(2):
                cols = slice(HALF * h, HALF * (h + 1))
                lcols = slice(LCOLS * h, LCOLS * (h + 1))
                nc.scalar.activation(
                    ea[:, t, cols], win[:].indirect(n4_l[:, lcols]), ACT.Exp,
                    bias=ea_bias[:, t : t + 1], scale=tau_c[:, t : t + 1],
                )
        for t in range(PACK):
            for h in range(2):
                cols = slice(HALF * h, HALF * (h + 1))
                lcols = slice(LCOLS * h, LCOLS * (h + 1))
                nc.vector.tensor_copy(s3[:, t, cols], s_win[t][:].indirect(n3_l[:, lcols]))
        for t in range(PACK):
            nc.vector.tensor_tensor(diff[:, t, :], s_win[t][:], s3[:, t, :], ALU.subtract)

        out_rows = out_0.rearrange("(p t) n -> p t n", t=PACK)
        words_out = out_1[0].rearrange("p n t -> p (n t)").bitcast(I32)
        o_s = sb("o_s", [P, S], U8)
        for c in range(4):
            cols = slice(QUARTER * c, QUARTER * (c + 1))
            root = sb("root%d" % c, [P, PACK, QUARTER], F32)
            recip = sb("recip%d" % c, [P, PACK, QUARTER], F32)
            res = sb("res%d" % c, [P, PACK, QUARTER], F32)
            nc.scalar.activation(root[:], ea[:, :, cols], ACT.Abs_reciprocal_sqrt, bias=0.5, scale=2.0)
            nc.scalar.activation(recip[:], root[:], ACT.Square)
            nc.vector.tensor_tensor(res[:], diff[:, :, cols], recip[:], ALU.mult)
            nc.sync.dma_start(out_rows[:, :, cols], res[:])
            o_bf = sb("o_bf%d" % c, [P, QUARTER * PACK], BF16)
            nc.vector.tensor_copy(
                o_bf[:].rearrange("p (c i t) -> p c t i", i=4, t=PACK),
                res[:].rearrange("p t (c i) -> p c t i", i=4),
            )
            o_w = sb("o_w%d" % c, [P, QUARTER], I32)
            nc.vector.quantize_mx(out=o_w[:].bitcast(FP8X4), scales=o_s[:, cols], in_=o_bf[:])
            nc.scalar.dma_start(words_out[:, cols], o_w[:])
        for q in range(4):
            engine = nc.sync if q % 2 else nc.scalar
            engine.dma_start(out_2[0, 4 * q : 4 * q + 4, :].bitcast(I32), o_s[32 * q : 32 * q + 4, :].bitcast(I32))
